import numpy as np
import ml_dtypes


def mxq(x, axis, fmt="e4m3"):
    dtype, down = {"e4m3": (ml_dtypes.float8_e4m3fn, 7), "e5m2": (ml_dtypes.float8_e5m2, 14)}[fmt]
    v = np.moveaxis(np.asarray(x, np.float32).astype(ml_dtypes.bfloat16).astype(np.float64), axis, -1)
    blocks = v.reshape(v.shape[:-1] + (-1, 32))
    amax = np.abs(blocks).max(-1, keepdims=True)
    byte = np.maximum(np.where(amax > 0, np.frexp(amax)[1] - 1 + 127, 0) - down, 1)
    scale = np.exp2(byte - 127.0)
    codes = (blocks / scale).astype(np.float32).astype(dtype).astype(np.float64)
    return np.moveaxis((codes * scale).reshape(v.shape), -1, axis)


WIDE = False


def mx_kscale(k):
    if not WIDE:
        return np.ones(k)
    levels = np.array([10, -10, 5, -5, 0])
    if k % 512:
        return np.exp2(np.random.permutation(np.resize(levels, k // 32))).repeat(32)
    a = np.empty((k // 512, 16))
    for p in range(k // 512):
        a[p, :8] = np.random.permutation(np.resize(levels, 8))
        for g in range(8):
            far = levels[np.abs(levels - a[p, g]) >= 10]
            a[p, g + 8] = far[np.random.randint(len(far))]
    return np.exp2(a.ravel()).repeat(32)


def f64(x):
    return np.asarray(x).astype(np.float64)


def striped(idx):
    return np.tile(idx.reshape(-1, 16).T, (8, 1)).astype(np.uint16)


def unstriped(offs):
    return offs[:16].T.reshape(-1).astype(np.int64)


def striped8(idx):
    return np.concatenate([x.reshape(-1, 16).T for x in idx]).astype(np.uint16)


def runs(offs, k):
    lists = np.stack([offs[16 * r : 16 * r + 16].T.reshape(-1) for r in range(8)]).astype(np.int64)
    return lists[np.arange(k) % 512 // 64]


def pack_weight(w):
    k, n = w.shape
    w = f64(np.asarray(w, np.float32).astype(ml_dtypes.bfloat16)).reshape(k // 32, 32, n)
    amax = np.abs(w).max(1)
    byte = np.clip(np.where(amax > 0, np.frexp(amax)[1] - 1 + 127 - 7, 1), 1, 254)
    scaled = (w * np.exp2(127.0 - byte)[:, None, :]).reshape(k, n).astype(np.float32)
    words = np.ascontiguousarray(scaled.reshape(k // 512, 128, 4, n).transpose(0, 1, 3, 2)).astype(ml_dtypes.float8_e4m3fn).view(np.uint8)
    return words, np.ascontiguousarray(byte.astype(np.uint8).reshape(k // 512, 16, n))


def unpack_weight(words, scales):
    g, p, n, _ = words.shape
    vals = np.ascontiguousarray(words).view(ml_dtypes.float8_e4m3fn).astype(np.float64) * np.repeat(np.exp2(scales.astype(np.float64) - 127.0), 8, axis=1)[..., None]
    return vals.transpose(0, 1, 3, 2).reshape(g * 512, n)


def sigmoid(v):
    return 1.0 / (1.0 + np.exp(-np.maximum(v, -700.0)))

def planes(y):
    n, m = y.shape
    v = y.astype(np.float32).astype(ml_dtypes.bfloat16).astype(np.float64).reshape(n // 32, 32, m)
    top = np.abs(v).max(1)
    byte = np.clip(np.where(top > 0, np.frexp(top)[1] - 1 + 127 - 7, 1), 1, 254)
    codes = (v * np.exp2(127.0 - byte)[:, None, :]).reshape(n, m).astype(np.float32).astype(ml_dtypes.float8_e4m3fn).view(np.uint8)
    words = codes.reshape(n // 512, 128, 4, m).transpose(0, 1, 3, 2)
    return np.ascontiguousarray(words), np.ascontiguousarray(byte.astype(np.uint8).reshape(n // 512, 16, m))


K, T, S, G, H, C, U = 512, 1024, 256, 2048, 512, 512, 512


def setup_inputs():
    n = np.random.standard_normal
    s = mx_kscale(K)[:, None]
    packed_xT = pack_weight(n((K, T)) * s)
    packed_dT = pack_weight(n((K, G)) / s)
    perm = np.random.permutation(U)
    return {
        "x_words": packed_xT[0],
        "x_scales": packed_xT[1],
        "d_words": packed_dT[0],
        "d_scales": packed_dT[1],
        "sl": np.random.uniform(1.0, 2.0, (H, 1)).astype(np.float32),
        "th": (0.5 * n((H, 1))).astype(np.float32),
        "gs": (np.random.uniform(0.5, 1.5, (K, 1)) / s).astype(np.float32),
        "offs": striped(np.random.permutation(T)[:S]),
        "ka": striped8(np.random.randint(0, G, (8, H))),
        "kb": striped8(np.random.randint(0, G, (8, H))),
        "n1": striped8(np.stack([np.random.permutation(S) for _ in range(8)])),
        "n2": striped8(np.stack([np.random.permutation(S) for _ in range(8)])),
        "cand": striped(np.random.permutation(T)[:C]),
        "n3": striped(perm[:S]),
        "n4": striped(perm[S:]),
        "n5": striped(np.random.permutation(S)),
    }


def reference(x_words, x_scales, d_words, d_scales, sl, th, gs, offs, ka, kb, n1, n2, cand, n3, n4, n5):
    x_cand = unpack_weight(x_words, x_scales)[:, unstriped(cand)]
    d_ka = unpack_weight(d_words, d_scales)[np.arange(K)[:, None], runs(ka, K)]
    xq = unpack_weight(x_words, x_scales)[:, unstriped(offs)]
    d_kb = unpack_weight(d_words, d_scales)[np.arange(K)[:, None], runs(kb, K)]
    h = 0.0625 * (d_ka.T @ xq + d_kb.T @ xq)
    st = h - (h[np.arange(H)[:, None], runs(n1, H)])
    sg = sigmoid(f64(sl) * (st[np.arange(H)[:, None], runs(n2, H)] - f64(th)))
    z = f64(gs) * (h * sg)
    s = 0.0625 * ((x_cand.T @ mxq(z, 0, "e4m3")))
    nw = s - s[:, unstriped(n5)]
    ph = np.zeros((C, U))
    ph[:, unstriped(n3)] = s
    out = ph.copy()
    out[:, unstriped(n4)] = nw
    return (out,) + planes(out)

@@ -1,0 +1,222 @@
+from contextlib import ExitStack
+
+import concourse.mybir as mybir
+
+K, T, S, G, H, C, U = 512, 1024, 256, 2048, 512, 512, 512
+FLOPS = 2 * K * S * (2 * H + C)
+
+F32 = mybir.dt.float32
+BF16 = mybir.dt.bfloat16
+I32 = mybir.dt.int32
+U32 = mybir.dt.uint32
+U16 = mybir.dt.uint16
+U8 = mybir.dt.uint8
+FP8X4 = mybir.dt.float8_e4m3fn_x4
+ACT = mybir.ActivationFunctionType
+ALU = mybir.AluOpType
+
+P = 128
+PACK = 4
+HALF = S // 2
+LIST_COL = 16
+SIXTEENTH = 0.0625
+
+
+def list_slice(tile, start, count):
+    return tile[:, start // LIST_COL : (start + count) // LIST_COL]
+
+
+def tile_picked_aqcehqpagq_none_po_kernel(
+    tc, x_words, x_scales, d_words, d_scales, sl, th, gs, offs, ka, kb, n1, n2, cand, n3, n4, n5, out_0, out_1, out_2
+):
+    nc = tc.nc
+    with ExitStack() as ctx:
+        keep = ctx.enter_context(tc.tile_pool(name="keep", bufs=1))
+        reused = ctx.enter_context(tc.tile_pool(name="reused", bufs=1))
+        chain = ctx.enter_context(tc.tile_pool(name="chain", bufs=1))
+        psum = ctx.enter_context(tc.psum_pool(name="psum", bufs=1))
+
+        def load_list(name, src):
+            tile = keep.tile([P, src.shape[1]], U16, name=name)
+            nc.sync.dma_start(tile[:], src)
+            return tile
+
+        def load_words(name, src, width):
+            tile = keep.tile([P, width], U32, name=name, align_bytes=64)
+            nc.sync.dma_start(tile[:].bitcast(I32), src[0].rearrange("p n t -> p (n t)").bitcast(I32))
+            return tile
+
+        def load_rowwise(name, src, offset):
+            tile = reused.tile([P, PACK], F32, name=name, offset=offset)
+            nc.sync.dma_start(tile[:], src.rearrange("(p t) o -> p (t o)", t=PACK))
+            return tile
+
+        d_bytes = keep.tile([P, G], U8, name="d_bytes", align_bytes=64)
+        nc.sync.dma_start(d_bytes[:].bitcast(I32), d_scales[0].bitcast(I32).unsqueeze(1).broadcast_to([16, 8, G // 4]))
+        ka_l = load_list("ka_l", ka)
+        kb_l = load_list("kb_l", kb)
+        offs_l = load_list("offs_l", offs)
+        x_tab = load_words("x_tab", x_words, T)
+        d_tab = load_words("d_tab", d_words, G)
+        x_bytes = keep.tile([P, T], U8, name="x_bytes", align_bytes=64)
+        for q in range(4):
+            rows = x_scales[0, 4 * q : 4 * q + 4, :].bitcast(I32).unsqueeze(0).broadcast_to([8, 4, T // 4])
+            nc.sync.dma_start(x_bytes[32 * q : 32 * q + 32, :].bitcast(I32), rows)
+        n1_l = load_list("n1_l", n1)
+        cand_l = load_list("cand_l", cand)
+        n2_l = load_list("n2_l", n2)
+        n3_l = load_list("n3_l", n3)
+        n5_l = load_list("n5_l", n5)
+        n4_l = load_list("n4_l", n4)
+
+        warm_in = keep.tile([P, 1], F32, name="warm_in")
+        nc.vector.memset(warm_in[:], 0.0)
+        warm_out = keep.tile([P, 1], F32, name="warm_out")
+        nc.scalar.activation(warm_out[:], warm_in[:], ACT.Sigmoid)
+
+        d_planes = keep.tile([P, PACK, 2, P], U8, name="d_planes", align_bytes=64)
+        d_planes_flat = d_planes[:].rearrange("p t a m -> p (t a m)")
+        nc.vector.memset(d_planes_flat.bitcast(I32), 0)
+        picked_bytes = keep.tile([P, 2, H], U8, name="picked_bytes", align_bytes=64)
+        for a, lst in enumerate((ka_l, kb_l)):
+            nc.vector.tensor_copy(picked_bytes[:, a, :], d_bytes[:].indirect(lst[:]))
+        dealt_bytes = reused.tile([P, PACK, 2 * P], U8, name="dealt_bytes", align_bytes=64, offset=0)
+        nc.vector.tensor_copy(
+            dealt_bytes[:].rearrange("p t (c i) -> p c t i", i=16),
+            picked_bytes[:].rearrange("p a (c i t) -> p (a c) t i", i=16, t=PACK),
+        )
+        dealt_flat = dealt_bytes[:].rearrange("p t m -> p (t m)")
+        for b in range(4):
+            nc.scalar.dma_start(d_planes_flat[b:P:32, :].bitcast(I32), dealt_flat[8 * b : P : 32, :].bitcast(I32))
+        sl_t = load_rowwise("sl_t", sl, 0)
+        th_t = load_rowwise("th_t", th, 64)
+        gs_t = load_rowwise("gs_t", gs, 128)
+
+        def pick_dictionary_words(name, lst, offset):
+            picked = reused.tile([P, H], U32, name=name + "_picked", align_bytes=64, offset=offset)
+            nc.vector.tensor_copy(picked[:], d_tab[:].indirect(lst[:]))
+            dealt = keep.tile([P, PACK, P], U32, name=name + "_dealt", align_bytes=64)
+            nc.vector.tensor_copy(
+                dealt[:].rearrange("p t (c i) -> p c t i", i=4),
+                picked[:].rearrange("p (c i t) -> p c t i", i=4, t=PACK),
+            )
+            return dealt
+
+        xq_words = keep.tile([P, S], U32, name="xq_words", align_bytes=64)
+        nc.vector.tensor_copy(xq_words[:], x_tab[:].indirect(offs_l[:]))
+        xq_plane = keep.tile([P, S], U8, name="xq_plane", align_bytes=64)
+        nc.vector.tensor_copy(xq_plane[:], x_bytes[:].indirect(offs_l[:]))
+        ka_words = pick_dictionary_words("ka", ka_l, 1024)
+        kb_words = pick_dictionary_words("kb", kb_l, 3072)
+
+        h_acc = [psum.tile([P, S], F32, name="h_acc%d" % t) for t in range(PACK)]
+        for a, words in enumerate((ka_words, kb_words)):
+            for t in range(PACK):
+                nc.tensor.matmul_mx(
+                    out=h_acc[t][:],
+                    lhsT=words[:, t, :].bitcast(FP8X4),
+                    lhsT_scale=d_planes[:, t, a, :],
+                    rhs=xq_words[:].bitcast(FP8X4),
+                    rhs_scale=xq_plane[:],
+                    start=(a == 0),
+                    stop=(a == 1),
+                )
+
+        neg_bias = keep.tile([P, PACK], F32, name="neg_bias")
+        sl_th = keep.tile([P, PACK], F32, name="sl_th")
+        nc.gpsimd.tensor_tensor(sl_th[:], sl_t[:], th_t[:], ALU.mult)
+        nc.gpsimd.tensor_scalar(neg_bias[:], sl_th[:], -1.0, 0.0, ALU.mult, ALU.add)
+
+        cand_words = reused.tile([P, PACK, P], U32, name="cand_words", align_bytes=64, offset=3072 + C)
+        nc.vector.tensor_copy(cand_words[:].rearrange("p t m -> p m t"), x_tab[:].indirect(cand_l[:]))
+        cand_plane = reused.tile([P, PACK, P], U8, name="cand_plane", align_bytes=64, offset=3072)
+        nc.vector.tensor_copy(cand_plane[:].rearrange("p t m -> p m t"), x_bytes[:].indirect(cand_l[:]))
+
+        h_t, st_t = [], []
+        for t in range(PACK):
+            h = keep.tile([P, 2 * S], F32, name="h%d" % t)
+            nc.scalar.activation(h[:, 0:S], h_acc[t][:], ACT.Copy, scale=SIXTEENTH)
+            other = keep.tile([P, S], F32, name="h_n1_%d" % t)
+            nc.scalar.activation(other[:], h[:].indirect(n1_l[:]), ACT.Copy)
+            st = keep.tile([P, S], F32, name="st%d" % t)
+            nc.vector.tensor_tensor(st[:], h[:, 0:S], other[:], ALU.subtract)
+            h_t.append(h)
+            st_t.append(st)
+
+        s_acc = [psum.tile([P, S], F32, name="s_acc%d" % t) for t in range(PACK)]
+        s_t = [keep.tile([P, S + LIST_COL], F32, name="s%d" % t) for t in range(PACK)]
+        page = [keep.tile([P, U], F32, name="page%d" % t) for t in range(PACK)]
+        for u in range(2):
+            cols = slice(u * HALF, (u + 1) * HALF)
+            z32 = chain.tile([P, PACK, HALF], F32, name="z32_%d" % u, align_bytes=64, offset=(0, 2048)[u])
+            z_rounded = chain.tile([P, HALF, PACK], BF16, name="z_rounded%d" % u, align_bytes=64, offset=(2048, 4096)[u])
+            for t in range(PACK):
+                sg = keep.tile([P, HALF], F32, name="sg%d_%d" % (u, t))
+                nc.scalar.activation(
+                    sg[:],
+                    st_t[t][:].indirect(list_slice(n2_l, u * HALF, HALF)),
+                    ACT.Sigmoid,
+                    bias=neg_bias[:, t : t + 1],
+                    scale=sl_t[:, t : t + 1],
+                )
+                nc.vector.scalar_tensor_tensor(z32[:, t, :], h_t[t][:, cols], gs_t[:, t : t + 1], sg[:], ALU.mult, ALU.mult)
+            nc.vector.tensor_copy(
+                z_rounded[:].rearrange("p (c i) t -> p c t i", i=4),
+                z32[:].rearrange("p t (c i) -> p c t i", i=4),
+            )
+            z_words = chain.tile([P, HALF], U32, name="z_words%d" % u, align_bytes=64, offset=(4096, 5120)[u])
+            z_plane = keep.tile([P, HALF], U8, name="z_plane%d" % u, align_bytes=64)
+            nc.vector.quantize_mx(
+                out=z_words[:].bitcast(FP8X4), scales=z_plane[:], in_=z_rounded[:].rearrange("p c t -> p (c t)")
+            )
+            for t in range(PACK):
+                nc.tensor.matmul_mx(
+                    out=s_acc[t][:, cols],
+                    lhsT=cand_words[:, t, :].bitcast(FP8X4),
+                    lhsT_scale=cand_plane[:, t, :],
+                    rhs=z_words[:].bitcast(FP8X4),
+                    rhs_scale=z_plane[:],
+                    start=True,
+                    stop=True,
+                )
+            for t in range(PACK):
+                nc.vector.tensor_scalar(s_t[t][:, cols], s_acc[t][:, cols], SIXTEENTH, None, ALU.mult)
+                if u == 0:
+                    nc.scalar.activation(page[t][:].indirect(list_slice(n3_l, 0, HALF)), s_t[t][:, cols], ACT.Copy)
+
+        y_rounded = keep.tile([P, U, PACK], BF16, name="y_rounded", align_bytes=64)
+        out_rows = out_0.rearrange("(p t) c -> p t c", t=PACK)
+        nw_t = []
+
+        def finish(t):
+            nc.scalar.activation(page[t][:].indirect(n4_l[:]), nw_t[t][:], ACT.Copy)
+            nc.sync.dma_start(out_rows[:, t, :], page[t][:])
+
+        for t in range(PACK):
+            other = keep.tile([P, S], F32, name="s_n5_%d" % t)
+            nc.scalar.activation(other[:], s_t[t][:].indirect(n5_l[:]), ACT.Copy)
+            nw = keep.tile([P, S], F32, name="nw%d" % t)
+            nc.vector.tensor_tensor(nw[:], s_t[t][:, 0:S], other[:], ALU.subtract)
+            nw_t.append(nw)
+            nc.scalar.activation(page[t][:].indirect(list_slice(n3_l, HALF, HALF)), s_t[t][:, HALF:S], ACT.Copy)
+            if t > 0:
+                finish(t - 1)
+                nc.vector.tensor_copy(y_rounded[:, :, t - 1], page[t - 1][:])
+        finish(PACK - 1)
+
+        y_words = keep.tile([P, U], U32, name="y_words", align_bytes=64)
+        y_plane = keep.tile([P, U], U8, name="y_plane", align_bytes=64)
+        words_out = out_1[0].rearrange("p n t -> p (n t)").bitcast(I32)
+        halves = (slice(0, U // 2), slice(U // 2, U))
+        for cols in halves:
+            nc.vector.tensor_copy(y_rounded[:, cols, PACK - 1], page[PACK - 1][:, cols])
+        for cols in halves:
+            nc.vector.quantize_mx(
+                out=y_words[:, cols].bitcast(FP8X4),
+                scales=y_plane[:, cols],
+                in_=y_rounded[:, cols, :].rearrange("p c t -> p (c t)"),
+            )
+            nc.sync.dma_start(words_out[:, cols], y_words[:, cols].bitcast(I32))
+        for q in range(4):
+            queue = nc.scalar if q < 2 else nc.sync
+            queue.dma_start(out_2[0, 4 * q : 4 * q + 4, :].bitcast(I32), y_plane[32 * q : 32 * q + 4, :].bitcast(I32))

@@ -17,13 +17,37 @@ ALU = mybir.AluOpType
 
 P = 128
 PACK = 4
+QUADRANT = 32
+BLOCKS = K // 32
+BLOCK_PARTITIONS = P // BLOCKS
+LIST_COLUMN = 16
+LINE = 16
 HALF = S // 2
-LIST_COL = 16
 SIXTEENTH = 0.0625
+
+PAGE_ORDER = (2, 0, 1, 3)
+
+DEALT_BYTES_AT = 0
+ROW_VECTOR_AT = {"sl": 0, "th": 64, "gs": 128}
+KA_PICKED_AT = DEALT_BYTES_AT + 2 * H
+KB_PICKED_AT = KA_PICKED_AT + 4 * H
+CAND_BYTES_AT = KB_PICKED_AT
+CAND_WORDS_AT = CAND_BYTES_AT + C
+
+Z_ROUNDED_BYTES = 2 * PACK * HALF
+Z_ROUNDED_AT = (0, Z_ROUNDED_BYTES)
+Z_WORDS_AT = (Z_ROUNDED_BYTES, 2 * Z_ROUNDED_BYTES)
 
 
 def list_slice(tile, start, count):
-    return tile[:, start // LIST_COL : (start + count) // LIST_COL]
+    return tile[:, start // LIST_COLUMN : (start + count) // LIST_COLUMN]
+
+
+def deal(nc, dealt, picked, run):
+    nc.vector.tensor_copy(
+        dealt.rearrange("p t (c i) -> p c t i", i=run),
+        picked.rearrange("p (c i t) -> p c t i", i=run, t=PACK),
+    )
 
 
 def tile_picked_aqcehqpagq_none_po_kernel(
@@ -33,7 +57,7 @@ def tile_picked_aqcehqpagq_none_po_kernel(
     with ExitStack() as ctx:
         keep = ctx.enter_context(tc.tile_pool(name="keep", bufs=1))
         reused = ctx.enter_context(tc.tile_pool(name="reused", bufs=1))
-        chain = ctx.enter_context(tc.tile_pool(name="chain", bufs=1))
+        halves = ctx.enter_context(tc.tile_pool(name="halves", bufs=1))
         psum = ctx.enter_context(tc.psum_pool(name="psum", bufs=1))
 
         def load_list(name, src):
@@ -46,22 +70,23 @@ def tile_picked_aqcehqpagq_none_po_kernel(
             nc.sync.dma_start(tile[:].bitcast(I32), src[0].rearrange("p n t -> p (n t)").bitcast(I32))
             return tile
 
-        def load_rowwise(name, src, offset):
-            tile = reused.tile([P, PACK], F32, name=name, offset=offset)
+        def load_row_vector(name, src):
+            tile = reused.tile([P, PACK], F32, name=name + "_t", offset=ROW_VECTOR_AT[name])
             nc.sync.dma_start(tile[:], src.rearrange("(p t) o -> p (t o)", t=PACK))
             return tile
 
         d_bytes = keep.tile([P, G], U8, name="d_bytes", align_bytes=64)
-        nc.sync.dma_start(d_bytes[:].bitcast(I32), d_scales[0].bitcast(I32).unsqueeze(1).broadcast_to([16, 8, G // 4]))
+        d_rows = d_scales[0].bitcast(I32).unsqueeze(1).broadcast_to([BLOCKS, BLOCK_PARTITIONS, G // 4])
+        nc.sync.dma_start(d_bytes[:].bitcast(I32), d_rows)
         ka_l = load_list("ka_l", ka)
         kb_l = load_list("kb_l", kb)
         offs_l = load_list("offs_l", offs)
         x_tab = load_words("x_tab", x_words, T)
-        d_tab = load_words("d_tab", d_words, G)
         x_bytes = keep.tile([P, T], U8, name="x_bytes", align_bytes=64)
-        for q in range(4):
-            rows = x_scales[0, 4 * q : 4 * q + 4, :].bitcast(I32).unsqueeze(0).broadcast_to([8, 4, T // 4])
-            nc.sync.dma_start(x_bytes[32 * q : 32 * q + 32, :].bitcast(I32), rows)
+        for q in range(P // QUADRANT):
+            rows = x_scales[0, 4 * q : 4 * q + 4, :].bitcast(I32).unsqueeze(0).broadcast_to([QUADRANT // 4, 4, T // 4])
+            nc.sync.dma_start(x_bytes[QUADRANT * q : QUADRANT * (q + 1), :].bitcast(I32), rows)
+        d_tab = load_words("d_tab", d_words, G)
         n1_l = load_list("n1_l", n1)
         cand_l = load_list("cand_l", cand)
         n2_l = load_list("n2_l", n2)
@@ -80,38 +105,35 @@ def tile_picked_aqcehqpagq_none_po_kernel(
         picked_bytes = keep.tile([P, 2, H], U8, name="picked_bytes", align_bytes=64)
         for a, lst in enumerate((ka_l, kb_l)):
             nc.vector.tensor_copy(picked_bytes[:, a, :], d_bytes[:].indirect(lst[:]))
-        dealt_bytes = reused.tile([P, PACK, 2 * P], U8, name="dealt_bytes", align_bytes=64, offset=0)
-        nc.vector.tensor_copy(
-            dealt_bytes[:].rearrange("p t (c i) -> p c t i", i=16),
-            picked_bytes[:].rearrange("p a (c i t) -> p (a c) t i", i=16, t=PACK),
-        )
+        dealt_bytes = reused.tile([P, PACK, 2 * P], U8, name="dealt_bytes", align_bytes=64, offset=DEALT_BYTES_AT)
+        deal(nc, dealt_bytes[:], picked_bytes[:].rearrange("p a h -> p (a h)"), LINE)
         dealt_flat = dealt_bytes[:].rearrange("p t m -> p (t m)")
         for b in range(4):
-            nc.scalar.dma_start(d_planes_flat[b:P:32, :].bitcast(I32), dealt_flat[8 * b : P : 32, :].bitcast(I32))
-        sl_t = load_rowwise("sl_t", sl, 0)
-        th_t = load_rowwise("th_t", th, 64)
-        gs_t = load_rowwise("gs_t", gs, 128)
+            nc.scalar.dma_start(
+                d_planes_flat[b:P:QUADRANT, :].bitcast(I32),
+                dealt_flat[BLOCK_PARTITIONS * b : P : QUADRANT, :].bitcast(I32),
+            )
+        sl_t = load_row_vector("sl", sl)
+        th_t = load_row_vector("th", th)
+        gs_t = load_row_vector("gs", gs)
 
         def pick_dictionary_words(name, lst, offset):
             picked = reused.tile([P, H], U32, name=name + "_picked", align_bytes=64, offset=offset)
             nc.vector.tensor_copy(picked[:], d_tab[:].indirect(lst[:]))
             dealt = keep.tile([P, PACK, P], U32, name=name + "_dealt", align_bytes=64)
-            nc.vector.tensor_copy(
-                dealt[:].rearrange("p t (c i) -> p c t i", i=4),
-                picked[:].rearrange("p (c i t) -> p c t i", i=4, t=PACK),
-            )
+            deal(nc, dealt[:], picked[:], LINE // 4)
             return dealt
 
         xq_words = keep.tile([P, S], U32, name="xq_words", align_bytes=64)
         nc.vector.tensor_copy(xq_words[:], x_tab[:].indirect(offs_l[:]))
         xq_plane = keep.tile([P, S], U8, name="xq_plane", align_bytes=64)
         nc.vector.tensor_copy(xq_plane[:], x_bytes[:].indirect(offs_l[:]))
-        ka_words = pick_dictionary_words("ka", ka_l, 1024)
-        kb_words = pick_dictionary_words("kb", kb_l, 3072)
+        ka_words = pick_dictionary_words("ka", ka_l, KA_PICKED_AT)
+        kb_words = pick_dictionary_words("kb", kb_l, KB_PICKED_AT)
 
         h_acc = [psum.tile([P, S], F32, name="h_acc%d" % t) for t in range(PACK)]
-        for a, words in enumerate((ka_words, kb_words)):
-            for t in range(PACK):
+        for t in range(PACK):
+            for a, words in enumerate((ka_words, kb_words)):
                 nc.tensor.matmul_mx(
                     out=h_acc[t][:],
                     lhsT=words[:, t, :].bitcast(FP8X4),
@@ -127,49 +149,58 @@ def tile_picked_aqcehqpagq_none_po_kernel(
         nc.gpsimd.tensor_tensor(sl_th[:], sl_t[:], th_t[:], ALU.mult)
         nc.gpsimd.tensor_scalar(neg_bias[:], sl_th[:], -1.0, 0.0, ALU.mult, ALU.add)
 
-        cand_words = reused.tile([P, PACK, P], U32, name="cand_words", align_bytes=64, offset=3072 + C)
-        nc.vector.tensor_copy(cand_words[:].rearrange("p t m -> p m t"), x_tab[:].indirect(cand_l[:]))
-        cand_plane = reused.tile([P, PACK, P], U8, name="cand_plane", align_bytes=64, offset=3072)
-        nc.vector.tensor_copy(cand_plane[:].rearrange("p t m -> p m t"), x_bytes[:].indirect(cand_l[:]))
+        cand_picked = reused.tile([P, C], U32, name="cand_picked", align_bytes=64, offset=CAND_WORDS_AT)
+        nc.vector.tensor_copy(cand_picked[:], x_tab[:].indirect(cand_l[:]))
+        cand_picked_bytes = reused.tile([P, C], U8, name="cand_picked_bytes", align_bytes=64, offset=CAND_BYTES_AT)
+        nc.vector.tensor_copy(cand_picked_bytes[:], x_bytes[:].indirect(cand_l[:]))
+        cand_words = keep.tile([P, PACK, P], U32, name="cand_words", align_bytes=64)
+        deal(nc, cand_words[:], cand_picked[:], LINE // 4)
+        cand_plane = keep.tile([P, PACK, P], U8, name="cand_plane", align_bytes=64)
+        deal(nc, cand_plane[:], cand_picked_bytes[:], LINE)
 
-        h_t, st_t = [], []
+        st_t = []
+        weighted = keep.tile([P, PACK, S], F32, name="weighted")
+        h_t = [keep.tile([P, 2 * S], F32, name="h%d" % t) for t in range(PACK)]
+        nc.scalar.activation(h_t[0][:, 0:S], h_acc[0][:], ACT.Copy, scale=SIXTEENTH)
         for t in range(PACK):
-            h = keep.tile([P, 2 * S], F32, name="h%d" % t)
-            nc.scalar.activation(h[:, 0:S], h_acc[t][:], ACT.Copy, scale=SIXTEENTH)
-            other = keep.tile([P, S], F32, name="h_n1_%d" % t)
-            nc.scalar.activation(other[:], h[:].indirect(n1_l[:]), ACT.Copy)
+            if t + 1 < PACK:
+                nc.scalar.activation(h_t[t + 1][:, 0:S], h_acc[t + 1][:], ACT.Copy, scale=SIXTEENTH)
+            h_n1 = keep.tile([P, S], F32, name="h_n1_%d" % t)
+            nc.scalar.activation(h_n1[:], h_t[t][:].indirect(n1_l[:]), ACT.Copy)
             st = keep.tile([P, S], F32, name="st%d" % t)
-            nc.vector.tensor_tensor(st[:], h[:, 0:S], other[:], ALU.subtract)
-            h_t.append(h)
+            nc.vector.tensor_tensor(st[:], h_t[t][:, 0:S], h_n1[:], ALU.subtract)
+            nc.vector.tensor_scalar(weighted[:, t, :], h_t[t][:, 0:S], gs_t[:, t : t + 1], None, ALU.mult)
             st_t.append(st)
 
         s_acc = [psum.tile([P, S], F32, name="s_acc%d" % t) for t in range(PACK)]
-        s_t = [keep.tile([P, S + LIST_COL], F32, name="s%d" % t) for t in range(PACK)]
+        s_t = [keep.tile([P, S + LIST_COLUMN], F32, name="s%d" % t) for t in range(PACK)]
         page = [keep.tile([P, U], F32, name="page%d" % t) for t in range(PACK)]
         for u in range(2):
             cols = slice(u * HALF, (u + 1) * HALF)
-            z32 = chain.tile([P, PACK, HALF], F32, name="z32_%d" % u, align_bytes=64, offset=(0, 2048)[u])
-            z_rounded = chain.tile([P, HALF, PACK], BF16, name="z_rounded%d" % u, align_bytes=64, offset=(2048, 4096)[u])
+            sg = keep.tile([P, PACK, HALF], F32, name="sg%d" % u)
+            z_rounded = halves.tile(
+                [P, HALF, PACK], BF16, name="z_rounded%d" % u, align_bytes=64, offset=Z_ROUNDED_AT[u]
+            )
             for t in range(PACK):
-                sg = keep.tile([P, HALF], F32, name="sg%d_%d" % (u, t))
                 nc.scalar.activation(
-                    sg[:],
+                    sg[:, t, :],
                     st_t[t][:].indirect(list_slice(n2_l, u * HALF, HALF)),
                     ACT.Sigmoid,
                     bias=neg_bias[:, t : t + 1],
                     scale=sl_t[:, t : t + 1],
                 )
-                nc.vector.scalar_tensor_tensor(z32[:, t, :], h_t[t][:, cols], gs_t[:, t : t + 1], sg[:], ALU.mult, ALU.mult)
-            nc.vector.tensor_copy(
-                z_rounded[:].rearrange("p (c i) t -> p c t i", i=4),
-                z32[:].rearrange("p t (c i) -> p c t i", i=4),
+            nc.vector.tensor_tensor(
+                z_rounded[:].rearrange("p (c i) t -> p c t i", i=LINE // 4),
+                weighted[:, :, cols].rearrange("p t (c i) -> p c t i", i=LINE // 4),
+                sg[:].rearrange("p t (c i) -> p c t i", i=LINE // 4),
+                ALU.mult,
             )
-            z_words = chain.tile([P, HALF], U32, name="z_words%d" % u, align_bytes=64, offset=(4096, 5120)[u])
+            z_words = halves.tile([P, HALF], U32, name="z_words%d" % u, align_bytes=64, offset=Z_WORDS_AT[u])
             z_plane = keep.tile([P, HALF], U8, name="z_plane%d" % u, align_bytes=64)
             nc.vector.quantize_mx(
                 out=z_words[:].bitcast(FP8X4), scales=z_plane[:], in_=z_rounded[:].rearrange("p c t -> p (c t)")
             )
-            for t in range(PACK):
+            for t in PAGE_ORDER:
                 nc.tensor.matmul_mx(
                     out=s_acc[t][:, cols],
                     lhsT=cand_words[:, t, :].bitcast(FP8X4),
@@ -179,44 +210,49 @@ def tile_picked_aqcehqpagq_none_po_kernel(
                     start=True,
                     stop=True,
                 )
-            for t in range(PACK):
+            for t in PAGE_ORDER:
                 nc.vector.tensor_scalar(s_t[t][:, cols], s_acc[t][:, cols], SIXTEENTH, None, ALU.mult)
                 if u == 0:
                     nc.scalar.activation(page[t][:].indirect(list_slice(n3_l, 0, HALF)), s_t[t][:, cols], ACT.Copy)
 
-        y_rounded = keep.tile([P, U, PACK], BF16, name="y_rounded", align_bytes=64)
+        page_rounded = keep.tile([P, U, PACK], BF16, name="page_rounded", align_bytes=64)
         out_rows = out_0.rearrange("(p t) c -> p t c", t=PACK)
-        nw_t = []
+        nw_t = {}
 
-        def finish(t):
+        def scatter_nw_and_store(t):
             nc.scalar.activation(page[t][:].indirect(n4_l[:]), nw_t[t][:], ACT.Copy)
             nc.sync.dma_start(out_rows[:, t, :], page[t][:])
 
-        for t in range(PACK):
-            other = keep.tile([P, S], F32, name="s_n5_%d" % t)
-            nc.scalar.activation(other[:], s_t[t][:].indirect(n5_l[:]), ACT.Copy)
+        for step, t in enumerate(PAGE_ORDER):
+            s_n5 = keep.tile([P, S], F32, name="s_n5_%d" % t)
+            nc.scalar.activation(s_n5[:], s_t[t][:].indirect(n5_l[:]), ACT.Copy)
             nw = keep.tile([P, S], F32, name="nw%d" % t)
-            nc.vector.tensor_tensor(nw[:], s_t[t][:, 0:S], other[:], ALU.subtract)
-            nw_t.append(nw)
+            nc.vector.tensor_tensor(nw[:], s_t[t][:, 0:S], s_n5[:], ALU.subtract)
+            nw_t[t] = nw
             nc.scalar.activation(page[t][:].indirect(list_slice(n3_l, HALF, HALF)), s_t[t][:, HALF:S], ACT.Copy)
-            if t > 0:
-                finish(t - 1)
-                nc.vector.tensor_copy(y_rounded[:, :, t - 1], page[t - 1][:])
-        finish(PACK - 1)
+            if step > 0:
+                before = PAGE_ORDER[step - 1]
+                scatter_nw_and_store(before)
+                nc.vector.tensor_copy(page_rounded[:, :, before], page[before][:])
+        last = PAGE_ORDER[-1]
+        scatter_nw_and_store(last)
 
-        y_words = keep.tile([P, U], U32, name="y_words", align_bytes=64)
-        y_plane = keep.tile([P, U], U8, name="y_plane", align_bytes=64)
+        page_words = keep.tile([P, U], U32, name="page_words", align_bytes=64)
+        page_plane = keep.tile([P, U], U8, name="page_plane", align_bytes=64)
         words_out = out_1[0].rearrange("p n t -> p (n t)").bitcast(I32)
-        halves = (slice(0, U // 2), slice(U // 2, U))
-        for cols in halves:
-            nc.vector.tensor_copy(y_rounded[:, cols, PACK - 1], page[PACK - 1][:, cols])
-        for cols in halves:
+        left, right = slice(0, U // 2), slice(U // 2, U)
+        nc.vector.tensor_copy(page_rounded[:, left, last], page[last][:, left])
+        nc.scalar.activation(page_rounded[:, right, last], page[last][:, right], ACT.Copy)
+        for cols in (left, right):
             nc.vector.quantize_mx(
-                out=y_words[:, cols].bitcast(FP8X4),
-                scales=y_plane[:, cols],
-                in_=y_rounded[:, cols, :].rearrange("p c t -> p (c t)"),
+                out=page_words[:, cols].bitcast(FP8X4),
+                scales=page_plane[:, cols],
+                in_=page_rounded[:, cols, :].rearrange("p c t -> p (c t)"),
             )
-            nc.sync.dma_start(words_out[:, cols], y_words[:, cols].bitcast(I32))
-        for q in range(4):
+            nc.sync.dma_start(words_out[:, cols], page_words[:, cols].bitcast(I32))
+        for q in range(P // QUADRANT):
             queue = nc.scalar if q < 2 else nc.sync
-            queue.dma_start(out_2[0, 4 * q : 4 * q + 4, :].bitcast(I32), y_plane[32 * q : 32 * q + 4, :].bitcast(I32))
+            queue.dma_start(
+                out_2[0, 4 * q : 4 * q + 4, :].bitcast(I32),
+                page_plane[QUADRANT * q : QUADRANT * q + 4, :].bitcast(I32),
+            )

from contextlib import ExitStack

import concourse.mybir as mybir

K, T, S, G, H, C, U = 512, 1024, 256, 2048, 512, 512, 512
FLOPS = 2 * K * S * (2 * H + C)

F32 = mybir.dt.float32
BF16 = mybir.dt.bfloat16
I32 = mybir.dt.int32
U32 = mybir.dt.uint32
U16 = mybir.dt.uint16
U8 = mybir.dt.uint8
FP8X4 = mybir.dt.float8_e4m3fn_x4
ACT = mybir.ActivationFunctionType
ALU = mybir.AluOpType

P = 128
PACK = 4
QUADRANT = 32
BLOCKS = K // 32
BLOCK_PARTITIONS = P // BLOCKS
LIST_COLUMN = 16
LINE = 16
HALF = S // 2
SIXTEENTH = 0.0625

PAGE_ORDER = (2, 0, 1, 3)

DEALT_BYTES_AT = 0
ROW_VECTOR_AT = {"sl": 0, "th": 64, "gs": 128}
KA_PICKED_AT = DEALT_BYTES_AT + 2 * H
KB_PICKED_AT = KA_PICKED_AT + 4 * H
CAND_BYTES_AT = KB_PICKED_AT
CAND_WORDS_AT = CAND_BYTES_AT + C

Z_ROUNDED_BYTES = 2 * PACK * HALF
Z_ROUNDED_AT = (0, Z_ROUNDED_BYTES)
Z_WORDS_AT = (Z_ROUNDED_BYTES, 2 * Z_ROUNDED_BYTES)


def list_slice(tile, start, count):
    return tile[:, start // LIST_COLUMN : (start + count) // LIST_COLUMN]


def deal(nc, dealt, picked, run):
    nc.vector.tensor_copy(
        dealt.rearrange("p t (c i) -> p c t i", i=run),
        picked.rearrange("p (c i t) -> p c t i", i=run, t=PACK),
    )


def tile_picked_aqcehqpagq_none_po_kernel(
    tc, x_words, x_scales, d_words, d_scales, sl, th, gs, offs, ka, kb, n1, n2, cand, n3, n4, n5, out_0, out_1, out_2
):
    nc = tc.nc
    with ExitStack() as ctx:
        keep = ctx.enter_context(tc.tile_pool(name="keep", bufs=1))
        reused = ctx.enter_context(tc.tile_pool(name="reused", bufs=1))
        halves = ctx.enter_context(tc.tile_pool(name="halves", bufs=1))
        psum = ctx.enter_context(tc.psum_pool(name="psum", bufs=1))

        def load_list(name, src):
            tile = keep.tile([P, src.shape[1]], U16, name=name)
            nc.sync.dma_start(tile[:], src)
            return tile

        def load_words(name, src, width):
            tile = keep.tile([P, width], U32, name=name, align_bytes=64)
            nc.sync.dma_start(tile[:].bitcast(I32), src[0].rearrange("p n t -> p (n t)").bitcast(I32))
            return tile

        def load_row_vector(name, src):
            tile = reused.tile([P, PACK], F32, name=name + "_t", offset=ROW_VECTOR_AT[name])
            nc.sync.dma_start(tile[:], src.rearrange("(p t) o -> p (t o)", t=PACK))
            return tile

        d_bytes = keep.tile([P, G], U8, name="d_bytes", align_bytes=64)
        d_rows = d_scales[0].bitcast(I32).unsqueeze(1).broadcast_to([BLOCKS, BLOCK_PARTITIONS, G // 4])
        nc.sync.dma_start(d_bytes[:].bitcast(I32), d_rows)
        ka_l = load_list("ka_l", ka)
        kb_l = load_list("kb_l", kb)
        offs_l = load_list("offs_l", offs)
        x_tab = load_words("x_tab", x_words, T)
        x_bytes = keep.tile([P, T], U8, name="x_bytes", align_bytes=64)
        for q in range(P // QUADRANT):
            rows = x_scales[0, 4 * q : 4 * q + 4, :].bitcast(I32).unsqueeze(0).broadcast_to([QUADRANT // 4, 4, T // 4])
            nc.sync.dma_start(x_bytes[QUADRANT * q : QUADRANT * (q + 1), :].bitcast(I32), rows)
        d_tab = load_words("d_tab", d_words, G)
        n1_l = load_list("n1_l", n1)
        cand_l = load_list("cand_l", cand)
        n2_l = load_list("n2_l", n2)
        n3_l = load_list("n3_l", n3)
        n5_l = load_list("n5_l", n5)
        n4_l = load_list("n4_l", n4)

        warm_in = keep.tile([P, 1], F32, name="warm_in")
        nc.vector.memset(warm_in[:], 0.0)
        warm_out = keep.tile([P, 1], F32, name="warm_out")
        nc.scalar.activation(warm_out[:], warm_in[:], ACT.Sigmoid)

        d_planes = keep.tile([P, PACK, 2, P], U8, name="d_planes", align_bytes=64)
        d_planes_flat = d_planes[:].rearrange("p t a m -> p (t a m)")
        nc.vector.memset(d_planes_flat.bitcast(I32), 0)
        picked_bytes = keep.tile([P, 2, H], U8, name="picked_bytes", align_bytes=64)
        for a, lst in enumerate((ka_l, kb_l)):
            nc.vector.tensor_copy(picked_bytes[:, a, :], d_bytes[:].indirect(lst[:]))
        dealt_bytes = reused.tile([P, PACK, 2 * P], U8, name="dealt_bytes", align_bytes=64, offset=DEALT_BYTES_AT)
        deal(nc, dealt_bytes[:], picked_bytes[:].rearrange("p a h -> p (a h)"), LINE)
        dealt_flat = dealt_bytes[:].rearrange("p t m -> p (t m)")
        for b in range(4):
            nc.scalar.dma_start(
                d_planes_flat[b:P:QUADRANT, :].bitcast(I32),
                dealt_flat[BLOCK_PARTITIONS * b : P : QUADRANT, :].bitcast(I32),
            )
        sl_t = load_row_vector("sl", sl)
        th_t = load_row_vector("th", th)
        gs_t = load_row_vector("gs", gs)

        def pick_dictionary_words(name, lst, offset):
            picked = reused.tile([P, H], U32, name=name + "_picked", align_bytes=64, offset=offset)
            nc.vector.tensor_copy(picked[:], d_tab[:].indirect(lst[:]))
            dealt = keep.tile([P, PACK, P], U32, name=name + "_dealt", align_bytes=64)
            deal(nc, dealt[:], picked[:], LINE // 4)
            return dealt

        xq_words = keep.tile([P, S], U32, name="xq_words", align_bytes=64)
        nc.vector.tensor_copy(xq_words[:], x_tab[:].indirect(offs_l[:]))
        xq_plane = keep.tile([P, S], U8, name="xq_plane", align_bytes=64)
        nc.vector.tensor_copy(xq_plane[:], x_bytes[:].indirect(offs_l[:]))
        ka_words = pick_dictionary_words("ka", ka_l, KA_PICKED_AT)
        kb_words = pick_dictionary_words("kb", kb_l, KB_PICKED_AT)

        h_acc = [psum.tile([P, S], F32, name="h_acc%d" % t) for t in range(PACK)]
        for t in range(PACK):
            for a, words in enumerate((ka_words, kb_words)):
                nc.tensor.matmul_mx(
                    out=h_acc[t][:],
                    lhsT=words[:, t, :].bitcast(FP8X4),
                    lhsT_scale=d_planes[:, t, a, :],
                    rhs=xq_words[:].bitcast(FP8X4),
                    rhs_scale=xq_plane[:],
                    start=(a == 0),
                    stop=(a == 1),
                )

        neg_bias = keep.tile([P, PACK], F32, name="neg_bias")
        sl_th = keep.tile([P, PACK], F32, name="sl_th")
        nc.gpsimd.tensor_tensor(sl_th[:], sl_t[:], th_t[:], ALU.mult)
        nc.gpsimd.tensor_scalar(neg_bias[:], sl_th[:], -1.0, 0.0, ALU.mult, ALU.add)

        cand_picked = reused.tile([P, C], U32, name="cand_picked", align_bytes=64, offset=CAND_WORDS_AT)
        nc.vector.tensor_copy(cand_picked[:], x_tab[:].indirect(cand_l[:]))
        cand_picked_bytes = reused.tile([P, C], U8, name="cand_picked_bytes", align_bytes=64, offset=CAND_BYTES_AT)
        nc.vector.tensor_copy(cand_picked_bytes[:], x_bytes[:].indirect(cand_l[:]))
        cand_words = keep.tile([P, PACK, P], U32, name="cand_words", align_bytes=64)
        deal(nc, cand_words[:], cand_picked[:], LINE // 4)
        cand_plane = keep.tile([P, PACK, P], U8, name="cand_plane", align_bytes=64)
        deal(nc, cand_plane[:], cand_picked_bytes[:], LINE)

        st_t = []
        weighted = keep.tile([P, PACK, S], F32, name="weighted")
        h_t = [keep.tile([P, 2 * S], F32, name="h%d" % t) for t in range(PACK)]
        nc.scalar.activation(h_t[0][:, 0:S], h_acc[0][:], ACT.Copy, scale=SIXTEENTH)
        for t in range(PACK):
            if t + 1 < PACK:
                nc.scalar.activation(h_t[t + 1][:, 0:S], h_acc[t + 1][:], ACT.Copy, scale=SIXTEENTH)
            h_n1 = keep.tile([P, S], F32, name="h_n1_%d" % t)
            nc.scalar.activation(h_n1[:], h_t[t][:].indirect(n1_l[:]), ACT.Copy)
            st = keep.tile([P, S], F32, name="st%d" % t)
            nc.vector.tensor_tensor(st[:], h_t[t][:, 0:S], h_n1[:], ALU.subtract)
            nc.vector.tensor_scalar(weighted[:, t, :], h_t[t][:, 0:S], gs_t[:, t : t + 1], None, ALU.mult)
            st_t.append(st)

        s_acc = [psum.tile([P, S], F32, name="s_acc%d" % t) for t in range(PACK)]
        s_t = [keep.tile([P, S + LIST_COLUMN], F32, name="s%d" % t) for t in range(PACK)]
        page = [keep.tile([P, U], F32, name="page%d" % t) for t in range(PACK)]
        for u in range(2):
            cols = slice(u * HALF, (u + 1) * HALF)
            sg = keep.tile([P, PACK, HALF], F32, name="sg%d" % u)
            z_rounded = halves.tile(
                [P, HALF, PACK], BF16, name="z_rounded%d" % u, align_bytes=64, offset=Z_ROUNDED_AT[u]
            )
            for t in range(PACK):
                nc.scalar.activation(
                    sg[:, t, :],
                    st_t[t][:].indirect(list_slice(n2_l, u * HALF, HALF)),
                    ACT.Sigmoid,
                    bias=neg_bias[:, t : t + 1],
                    scale=sl_t[:, t : t + 1],
                )
            nc.vector.tensor_tensor(
                z_rounded[:].rearrange("p (c i) t -> p c t i", i=LINE // 4),
                weighted[:, :, cols].rearrange("p t (c i) -> p c t i", i=LINE // 4),
                sg[:].rearrange("p t (c i) -> p c t i", i=LINE // 4),
                ALU.mult,
            )
            z_words = halves.tile([P, HALF], U32, name="z_words%d" % u, align_bytes=64, offset=Z_WORDS_AT[u])
            z_plane = keep.tile([P, HALF], U8, name="z_plane%d" % u, align_bytes=64)
            nc.vector.quantize_mx(
                out=z_words[:].bitcast(FP8X4), scales=z_plane[:], in_=z_rounded[:].rearrange("p c t -> p (c t)")
            )
            for t in PAGE_ORDER:
                nc.tensor.matmul_mx(
                    out=s_acc[t][:, cols],
                    lhsT=cand_words[:, t, :].bitcast(FP8X4),
                    lhsT_scale=cand_plane[:, t, :],
                    rhs=z_words[:].bitcast(FP8X4),
                    rhs_scale=z_plane[:],
                    start=True,
                    stop=True,
                )
            for t in PAGE_ORDER:
                nc.vector.tensor_scalar(s_t[t][:, cols], s_acc[t][:, cols], SIXTEENTH, None, ALU.mult)
                if u == 0:
                    nc.scalar.activation(page[t][:].indirect(list_slice(n3_l, 0, HALF)), s_t[t][:, cols], ACT.Copy)

        page_rounded = keep.tile([P, U, PACK], BF16, name="page_rounded", align_bytes=64)
        out_rows = out_0.rearrange("(p t) c -> p t c", t=PACK)
        nw_t = {}

        def scatter_nw_and_store(t):
            nc.scalar.activation(page[t][:].indirect(n4_l[:]), nw_t[t][:], ACT.Copy)
            nc.sync.dma_start(out_rows[:, t, :], page[t][:])

        for step, t in enumerate(PAGE_ORDER):
            s_n5 = keep.tile([P, S], F32, name="s_n5_%d" % t)
            nc.scalar.activation(s_n5[:], s_t[t][:].indirect(n5_l[:]), ACT.Copy)
            nw = keep.tile([P, S], F32, name="nw%d" % t)
            nc.vector.tensor_tensor(nw[:], s_t[t][:, 0:S], s_n5[:], ALU.subtract)
            nw_t[t] = nw
            nc.scalar.activation(page[t][:].indirect(list_slice(n3_l, HALF, HALF)), s_t[t][:, HALF:S], ACT.Copy)
            if step > 0:
                before = PAGE_ORDER[step - 1]
                scatter_nw_and_store(before)
                nc.vector.tensor_copy(page_rounded[:, :, before], page[before][:])
        last = PAGE_ORDER[-1]
        scatter_nw_and_store(last)

        page_words = keep.tile([P, U], U32, name="page_words", align_bytes=64)
        page_plane = keep.tile([P, U], U8, name="page_plane", align_bytes=64)
        words_out = out_1[0].rearrange("p n t -> p (n t)").bitcast(I32)
        left, right = slice(0, U // 2), slice(U // 2, U)
        nc.vector.tensor_copy(page_rounded[:, left, last], page[last][:, left])
        nc.scalar.activation(page_rounded[:, right, last], page[last][:, right], ACT.Copy)
        for cols in (left, right):
            nc.vector.quantize_mx(
                out=page_words[:, cols].bitcast(FP8X4),
                scales=page_plane[:, cols],
                in_=page_rounded[:, cols, :].rearrange("p c t -> p (c t)"),
            )
            nc.sync.dma_start(words_out[:, cols], page_words[:, cols].bitcast(I32))
        for q in range(P // QUADRANT):
            queue = nc.scalar if q < 2 else nc.sync
            queue.dma_start(
                out_2[0, 4 * q : 4 * q + 4, :].bitcast(I32),
                page_plane[QUADRANT * q : QUADRANT * q + 4, :].bitcast(I32),
            )
